import numpy as np, ml_dtypes
CORES = [83,85,87,115,117,119]
N = 6
BF = ml_dtypes.bfloat16
M, D, LV, CAP = 1024, 3, 5, 256
P, H = N * M, 2 ** LV - 1
def ancestors(t):
    p, s = t >> 1, t & 1
    L = np.full((8, P + 1), P, np.int64); R = L.copy()
    for k in range(LV):
        a = np.where(s == 1, p, np.take_along_axis(L, p, 1)); b = np.where(s == 0, p, np.take_along_axis(R, p, 1))
        L[:, :P] = a; R[:, :P] = b
    return L[:, :P], R[:, :P]
def wants(t):
    L, R = ancestors(t); w = np.zeros((8, N, P + 1), bool); g = np.arange(8)[:, None]; r = (np.arange(P) // M)[None]
    w[g, r, L] = True; w[g, r, R] = True
    return w[:, :, :P].reshape(8, N, N, M)
def fit(rng, t):
    w = wants(t); L, R = ancestors(t)
    for g, r, q in np.argwhere(np.count_nonzero(w, axis=3) > CAP):
        if r != q:
            c = rng.permutation(np.flatnonzero(w[g, r, q]))[CAP:] + q * M; a = r * M
            x = t[g, a:a + M]; x[np.isin(L[g, a:a + M], c) | np.isin(R[g, a:a + M], c)] = 2 * P
def grid(rng):
    lev = np.array([c.bit_length() - 1 for c in range(1, H + 1)]); k = rng.random((H,) * D); s = np.zeros((H,) * D, np.int64)
    for d in range(D):
        e = lev.reshape([H if i == d else 1 for i in range(D)]); s = s + e; k = k + (0.75 + 0.5 * rng.random()) * e
    for d in range(D):
        u = np.moveaxis(k, d, 0)
        for c in range(2, H + 1): u[c - 1] = np.maximum(u[c - 1], u[c // 2 - 1])
    o = np.lexsort((s.reshape(-1), k.reshape(-1)))[:P]; o = o[rng.permutation(P)]
    num = np.full(H ** D, P); num[o] = np.arange(P); c = np.stack(np.unravel_index(o, (H,) * D)) + 1
    t = np.full((D, P), 2 * P)
    for d in range(D):
        b = c.copy(); b[d] = np.maximum(b[d] // 2, 1)
        t[d] = np.where(c[d] > 1, 2 * num[np.ravel_multi_index(tuple(b - 1), (H,) * D)] + c[d] % 2, 2 * P)
    return t
def vals(rng):
    return (rng.standard_normal((N, 128, M), dtype=np.float32) * np.exp2(rng.integers(-2, 3, (N, 128, 1)))).astype(np.float32)
def made(rng, v, t):
    for d in range(D): fit(rng, t[:, d])
    return {"v": v, "tree": np.repeat(t.reshape(1, 8, D * P).astype(np.int32), N, axis=0)}
def heaps(o):
    b = o[:len(o) // H * H].reshape(-1, H); c = np.arange(2, H + 1)
    return b[:, 1:], 2 * b[:, c // 2 - 1] + c % 2
def setup_inputs(rng):
    return made(rng, vals(rng), np.stack([grid(rng) for g in range(8)]))
def setup_inputs_full(rng):
    t = np.full((8, D, P), 2 * P); n3 = min(CAP, M - 2 * CAP); n4 = max(0, min(CAP, M - 3 * CAP))
    for g, d in np.ndindex(8, D):
        o = np.stack([q * M + rng.permutation(M) for q in range(N)]); a = np.roll(o, -(1 + (g + d) % (N - 1)), axis=0)
        s = rng.integers(0, 2, (3, N, CAP)); x = t[g, d]
        x[o[:, CAP:2 * CAP]] = 2 * a[:, :CAP] + s[0]
        x[o[:, 2 * CAP:2 * CAP + n3]] = 2 * o[:, CAP:CAP + n3] + s[1][:, :n3]
        x[o[:, 3 * CAP:3 * CAP + n4]] = 2 * o[:, 2 * CAP:2 * CAP + n4] + s[2][:, :n4]
    return made(rng, vals(rng), t)
def setup_inputs_chains(rng):
    t = np.full((8, D, P), 2 * P); k = P // LV
    for g, d in np.ndindex(8, D):
        o = np.concatenate([[0, P - 1], 1 + rng.permutation(P - 2)])[:k * LV].reshape(k, LV)
        s = rng.integers(0, 2, (k, LV)); s[0] = 1; s[0, 1] = 0; s[1] = 0; s[1, 1] = 1
        x = t[g, d]; x[o[:, 1:]] = 2 * o[:, :-1] + s[:, 1:]
    return made(rng, vals(rng), t)
def setup_inputs_near(rng):
    t = np.full((8, D, P), 2 * P)
    for g, d in np.ndindex(8, D):
        x = t[g, d]
        if (g + d) % 3 == 1:
            for q in range(N):
                i, e = heaps(q * M + rng.permutation(M)); x[i] = e
        if (g + d) % 3 == 2:
            i, e = heaps(rng.permutation(P)); x[i] = e
    return made(rng, vals(rng), t)
def setup_inputs_spread(rng):
    d = setup_inputs(rng); k = (N, 1, M)
    d["v"] = (d["v"] * np.exp2(rng.integers(-6, 7, k)) * (rng.random(k) > 0.0625)).astype(np.float32); return d
def check_inputs(d):
    bad = []; a = np.abs(d["v"].astype(np.float64)); tr = d["tree"].astype(np.int64)
    if not ((a == 0) | ((a >= 2.0 ** -60) & (a <= 2.0 ** 60))).all(): bad.append("sizes")
    if (tr != tr[:1]).any(): bad.append("alike")
    if tr.min() < 0 or tr.max() > 2 * P: return bad + ["codes"]
    other = ~np.eye(N, dtype=bool)
    for k in range(D):
        t = tr[0][:, k * P:(k + 1) * P]
        for g in range(8):
            c = t[g][t[g] < 2 * P]; up = np.append(t[g] >> 1, P); x = np.arange(P)
            if len(np.unique(c)) < len(c): bad.append("sides")
            for i in range(LV): x = up[x]
            if (x != P).any(): bad.append("levels")
        if (np.count_nonzero(wants(t), axis=3)[:, other] > CAP).any(): bad.append("wanted")
    return sorted(set(bad))
def reference(v, tree):
    u = np.zeros((8, 16, P + 1), np.float32)
    u[:, :, :P] = v.reshape(N, 8, 16, M).transpose(1, 2, 0, 3).reshape(8, 16, P)
    for d in range(D):
        L, R = ancestors(tree[0][:, d * P:(d + 1) * P].astype(np.int64))
        for g in range(8):
            s = u[g][:, L[g]] + u[g][:, R[g]]
            u[g, :, :P] = u[g, :, :P] - np.float32(0.5) * s
    y = u[:, :, :P].reshape(8, 16, N, M).transpose(2, 0, 1, 3).reshape(N, 128, M)
    return {"y": np.ascontiguousarray(y)}

@@ -1,0 +1,468 @@
+from concourse.bass import DstId, RemoteDMATransfer
+from concourse.mybir import AluOpType, ActivationFunctionType
+
+M, P, ND = 1024, 6144, 3
+WW, IWW = P + 8, P + 16
+SEG = P // 16
+FILL = 516
+OPT = {
+    "ag": [128, 384, 384, 128],
+    "ch": [256, 256, 512, 512, 256, 256],
+    "last": [256, 256, 256, 256],
+    "relay": 1,
+    "pen": 128,
+    "p0": 608, "p3": 608, "pa": 512, "pb": 512,
+    "early": 0,
+    "vq": "ac",
+}
+
+SCRATCH = {
+    "W0": ("sbuf", [128, WW], "float32"), "W1": ("sbuf", [128, WW], "float32"), "W2": ("sbuf", [128, WW], "float32"),
+    "IW": ("sbuf", [128, IWW], "bfloat16"),
+    "CT": ("sbuf", [128, ND * SEG], "int32"),
+    "HI": ("sbuf", [128, ND * SEG], "bfloat16"), "LO": ("sbuf", [128, ND * SEG], "bfloat16"),
+    "R": ("sbuf", [128, 9 * M], "bfloat16"),
+    "A": ("sbuf", [128, 5 * M], "float32"), "S": ("sbuf", [128, 5 * M], "float32"),
+    "Y": ("sbuf", [128, M], "float32"), "Y2": ("sbuf", [128, M], "float32"),
+    "Z": ("sbuf", [128, ND * 144], "bfloat16"),
+    "HF": ("sbuf", [128, 32], "bfloat16"), "HG": ("sbuf", [128, 32], "bfloat16"),
+    "I2": ("sbuf", [128, 128], "float32"),
+    "NF0": ("sbuf", [128, 128], "uint16"), "NF1": ("sbuf", [128, 128], "uint16"), "NF2": ("sbuf", [128, 128], "uint16"),
+    "PF0": ("sbuf", [128, 128], "uint16"), "PF1": ("sbuf", [128, 128], "uint16"),
+    "Q": ("sbuf", [128, 6 * 64], "uint16"),
+    "DI": ("sbuf", [128, 12 * 64], "int32"),
+    "SM": ("sbuf", [128, 60 * 64], "float32"),
+}
+for _k in range(4):
+    SCRATCH["PS%d" % _k] = ("psum", [128, 512], "float32")
+    SCRATCH["PX%d" % _k] = ("psum", [128, 512], "float32")
+SEMAPHORES = (["ve", "ac", "pe", "po", "sent", "a0", "a1", "a2", "l0", "l1"] + ["h%d" % _k for _k in range(24)]
+              + ["d%d" % _k for _k in range(24)])
+
+
+def _starts(widths):
+    out, a = [], 0
+    for w in widths:
+        out.append((a, w))
+        a += w
+    return out
+
+
+def _layout(T, topo):
+    cores = list(T.cores)
+    chips = {}
+    for c in cores:
+        chips.setdefault(topo.chip(c), []).append(c)
+    one, two = list(chips.values())
+    partner, peers, inbound = {}, {}, {}
+    for mine, other in ((one, two), (two, one)):
+        free = [c for c in topo.cores_of(other[0]) if c not in cores]
+        for a, b in zip(mine, other):
+            partner[a] = b
+            peers[a] = [c for c in mine if c != a]
+            h = [c for c in free if topo.die(c) == topo.die(a) and topo.may_write(a, c)][0]
+            free.remove(h)
+            inbound[a] = h
+    calls, jobs, load = {c: {} for c in cores}, {}, {}
+
+    def through(h, eng, buf, lo, hi, dsts, sem):
+        j = jobs.setdefault(h, [])
+        j.append(("h%d" % len(j), len(eng), (buf, lo, hi, [(dsts, topo.engines(h, dsts[0]), sem)])))
+        return ([h], eng, j[-1][0])
+
+    for k, (a, w) in enumerate(_starts(OPT["ag"])):
+        for c in cores:
+            lo = T.rank_of(c) * M + a
+            h = min([x for x in topo.cores_of(partner[c]) if x not in cores and topo.may_write(c, x)],
+                    key=lambda x: load.get(x, 0) + (0 if x == inbound[c] else 1 if topo.die(x) == topo.die(c)
+                                                    else OPT["pen"]))
+            load[h] = load.get(h, 0) + w
+            off = topo.engines(c, h)
+            rest = [e for e in topo.engines(c, peers[c][0]) if e not in off]
+            far = through(h, off, "W0", lo, lo + w, [partner[c]] + peers[partner[c]], "a0")
+            calls[c]["ag", k] = ("W0", lo, lo + w, [far, (peers[c], rest, "a0")])
+    for d in (1, 2):
+        for k, (a, w) in enumerate([(0, 512)] + _starts(OPT["ch"])[2:]):
+            for c in cores:
+                lo = T.rank_of(c) * M + a if a < M else T.rank_of(partner[c]) * M + a - M
+                eng, buf, s = topo.engines(c, peers[c][0]), "W%d" % d, "a%d" % d
+                way = (through(inbound[partner[c]], eng, buf, lo, lo + w, peers[c], s) if k < OPT["relay"]
+                       else (peers[c], eng, s))
+                calls[c][d, k] = (buf, lo, lo + w, [way])
+    return partner, calls, jobs
+
+
+def _issue(g, T, topo, call):
+    buf, lo, hi, ways = call
+    ap, tr = T[buf][:, lo:hi], []
+    for dsts, eng, s in ways:
+        ids = [DstId(rid=topo.addr(x)[0], pnc=topo.addr(x)[1]) for x in dsts]
+        tr.append(RemoteDMATransfer(dst_ids=ids, dma_engine_mask=sum(1 << e for e in eng), remote_sem=T.sem[s],
+                                    srcs=[ap], dsts=[ap] * len(dsts)))
+    g.remote_dma_fused(tr, local_sem=T.sem["sent"])
+    return sum(len(w[1]) for w in ways)
+
+
+def rank_program(g, core, T, topo):
+    partner, calls, jobs = _layout(T, topo)
+    rank = T.rank_of(core)
+    if rank is None:
+        n = 0
+        for s, k, call in jobs.get(core, []):
+            g.wait_ge(T.sem[s], k)
+            n += _issue(g, T, topo, call)
+        if n:
+            g.wait_ge(T.sem["sent"], n)
+        return
+
+    own, par = rank * M, T.rank_of(partner[core]) * M
+    Q = {"ve": g.vector, "ac": g.scalar, "pe": g.tensor, "po": g, "sy": g.sync}
+    cnt = {"sent": 0}
+    seen = {q: {} for q in Q}
+    log = {}
+    bank = {}
+    ndma, nsm = [0], [0]
+    add, sub, mul = AluOpType.add, AluOpType.subtract, AluOpType.mult
+    ident = ActivationFunctionType.Identity
+
+    def wait(q, tok):
+        if seen[q].get(tok[0], 0) < tok[1]:
+            Q[q].wait_ge(T.sem[tok[0]], tok[1])
+            seen[q][tok[0]] = tok[1]
+
+    def before(q, reads, writes, banks):
+        need = {}
+        for rs, w in ((reads, False), (writes, True)):
+            for (b, lo, hi) in rs:
+                for (l2, h2, w2, tok) in log.get(b, []):
+                    if l2 < hi and lo < h2 and (w or w2):
+                        need[tok[0]] = max(need.get(tok[0], 0), tok[1])
+        for b in banks:
+            for q2, tok in bank.get(b, {}).items():
+                if q2 != q:
+                    need[tok[0]] = max(need.get(tok[0], 0), tok[1])
+        for s in need:
+            wait(q, (s, need[s]))
+
+    def after(q, reads, writes, banks, tok):
+        for rs, w in ((reads, False), (writes, True)):
+            for (b, lo, hi) in rs:
+                log.setdefault(b, []).append((lo, hi, w, tok))
+        for b in banks:
+            bank.setdefault(b, {})[q] = tok
+
+    def op(q, fn, reads=(), writes=(), banks=()):
+        before(q, reads, writes, banks)
+        cnt[q] = cnt.get(q, 0) + 1
+        fn().then_inc(T.sem[q], 1)
+        after(q, reads, writes, banks, (q, cnt[q]))
+
+    def dmas(q, pairs, reads=(), writes=()):
+        before(q, reads, writes, ())
+        s = "d%d" % ndma[0]
+        ndma[0] += 1
+        for out, in_ in pairs:
+            Q[q].dma_start(out, in_).then_inc(T.sem[s], 16)
+        cnt[s] = 16 * len(pairs)
+        after(q, reads, writes, (), (s, cnt[s]))
+
+    def send(tag):
+        call = calls[core][tag]
+        before("po", [call[0:3]], (), ())
+        cnt["sent"] += _issue(g, T, topo, call)
+
+    every = [x for c in calls for x in calls[c].values()] + [j[2] for h in jobs for j in jobs[h]]
+    here = [(buf, lo, hi, len(eng), s) for (buf, lo, hi, ways) in every for (dsts, eng, s) in ways if core in dsts]
+    for buf, lo, hi, n, s in here:
+        cnt[s] = cnt.get(s, 0) + n
+    for buf, lo, hi, n, s in here:
+        after("po", (), [(buf, lo, hi)], (), (s, cnt[s]))
+    for d in (0, 1):
+        cnt["l%d" % d] = len(topo.engines(partner[core], core))
+        after("po", (), [("PF%d" % d, 64, 128)], (), ("l%d" % d, cnt["l%d" % d]))
+
+    V, S_, PE = g.vector, g.scalar, g.tensor
+
+    dmas("sy", [(T.CT[:, 0:SEG], T.tree[:, 0:P])], writes=[("CT", 0, SEG)])
+    for a, w in _starts(OPT["ag"]):
+        dmas(OPT["vq"], [(T.W0[:, own + a:own + a + w], T.v[:, a:a + w])], writes=[("W0", own + a, own + a + w)])
+    dmas(OPT["vq"], [(T.CT[:, d * SEG:(d + 1) * SEG], T.tree[:, d * P:(d + 1) * P]) for d in (1, 2)],
+         writes=[("CT", SEG, ND * SEG)])
+    cut = IWW - 5 * FILL
+    op("ve", lambda: V.memset(T.IW[:, 0:FILL], float(P)), writes=[("IW", 0, FILL)])
+    op("ve", lambda: V.memset(T.HF[:, :], 0.5), writes=[("HF", 0, 32)])
+    op("ve", lambda: V.memset(T.Z[:, :], 0.0), writes=[("Z", 0, 432)])
+    op("ve", lambda: V.memset(T.I2[:, :], 2.0), writes=[("I2", 0, 128)])
+    op("ve", lambda: V.memset(T.IW[:, FILL:cut], float(P)), writes=[("IW", FILL, cut)])
+    for i in range(5):
+        a = cut + i * FILL
+        op("ac", lambda: S_.activation(T.IW[:, a:a + FILL], T.IW[:, 0:FILL], ident),
+           reads=[("IW", 0, FILL)], writes=[("IW", a, a + FILL)])
+    op("po", lambda: g.affine_select(T.HG[:, 0:27], T.HF[:, 0:27], [[-2, 3], [-16, 9]], AluOpType.is_ge, 0.0, 0, 1),
+       reads=[("HF", 0, 32)], writes=[("HG", 0, 32)])
+    op("po", lambda: g.affine_select(T.Z[:, 15::16], T.HG[:, 0:27], [[2, 3], [16, 9]], AluOpType.is_ge, 0.0, 1, -1),
+       reads=[("HG", 0, 32)], writes=[("Z", 0, 432)])
+    op("po", lambda: g.affine_select(T.I2[:, :], T.I2[:, :], [[-1, 128]], AluOpType.is_equal, 0.0, 0, 1),
+       reads=[("I2", 0, 128)], writes=[("I2", 0, 128)])
+
+    def digits(lo, hi):
+        op("ve", lambda: V.tensor_copy(T.HI[:, lo:hi], T.CT[:, lo:hi]), reads=[("CT", lo, hi)], writes=[("HI", lo, hi)])
+        op("ve", lambda: V.tensor_tensor(T.LO[:, lo:hi], T.CT[:, lo:hi], T.HI[:, lo:hi], sub),
+           reads=[("CT", lo, hi), ("HI", lo, hi)], writes=[("LO", lo, hi)])
+
+    def rows(ds):
+        pairs = []
+        for d in ds:
+            pairs.append((T.IW[2 * d::16, 0:P], T.HI[:, d * SEG:(d + 1) * SEG]))
+            pairs.append((T.IW[2 * d + 1::16, 0:P], T.LO[:, d * SEG:(d + 1) * SEG]))
+        lo, hi = ds[0] * SEG, (ds[-1] + 1) * SEG
+        dmas("sy", pairs, reads=[("HI", lo, hi), ("LO", lo, hi)], writes=[("IW", 0, P)])
+
+    def col(x):
+        return own + x if x < M else par + x - M
+
+    def twice(d, b):
+        c = col(512 * b)
+        op("pe", lambda: PE.matmul(T["PS%d" % b][:, 0:512], T.I2[:, :], T["W%d" % d][:, c:c + 512], True, True),
+           reads=[("I2", 0, 128), ("W%d" % d, c, c + 512)], banks=["PS%d" % b])
+
+    def X(d, k):
+        return T["PX%d" % k][:, 64 * d:64 * d + 64] if k < 4 else T.PX3[:, 192 + 64 * d:256 + 64 * d]
+
+    def wrap(d, k):
+        buf, a = ("IW", own) if k == 0 else ("IW", par) if k == 4 else ("R", (3 * d + k - 1) * M)
+        reads, banks = [(buf, a, a + M), ("Z", 0, 432)], ["PX%d" % min(k, 3)]
+        before("pe", reads, (), banks)
+        for o in range(15):
+            PE.matmul(X(d, k), T.Z[:, 144 * d + 15 - o:144 * d + 143 - o], T[buf][:, a + o:a + M:16], o == 0, False)
+        op("pe", lambda: PE.matmul(X(d, k), T.Z[:, 144 * d:144 * d + 128], T[buf][:, a + 15:a + M:16], False, True),
+           reads=reads, banks=banks)
+
+    def offs(d, k):
+        return ("NF%d" % d, 0) if k == 0 else ("PF%d" % d, 0) if k == 4 else ("Q", (2 * d + k - 1) * 64)
+
+    def parents(d, k):
+        b, a = offs(d, k)
+        op("ve", lambda: V.tensor_scalar(T[b][:, a:a + 64], X(d, k), -0.25, None, add),
+           writes=[(b, a, a + 64)], banks=["PX%d" % min(k, 3)])
+
+    def chase(q, d, k, lo, hi):
+        if lo == hi:
+            return
+        b, a = offs(d, k - 1)
+        r = (3 * d + k - 1) * M
+        src = T.IW[:, 0:IWW].indirect(T[b][:, a + lo // 16:a + hi // 16])
+        out = T.R[:, r + lo:r + hi]
+        fn = (lambda: S_.activation(out, src, ident)) if q == "ac" else (lambda: V.tensor_copy(out, src))
+        op(q, fn, reads=[("IW", 0, IWW), (b, a + lo // 16, a + hi // 16)], writes=[("R", r + lo, r + hi)])
+
+    def slot():
+        nsm[0] += 1
+        a = (nsm[0] - 1) * 64
+        return T.SM[:, a:a + 64], ("SM", a, a + 64)
+
+    st = {}
+
+    def tt(x, y, alu):
+        o = slot()
+        op("ve", lambda: V.tensor_tensor(o[0], x[0], y[0], alu), reads=[x[1], y[1]], writes=[o[1]])
+        return o
+
+    def flags(d, k):
+        a = (4 * d + k) * 64
+        D = (T.DI[:, a:a + 64], ("DI", a, a + 64))
+        op("ve", lambda: V.tensor_scalar(D[0], X(d, k), -(P + 0.25), None, add), writes=[D[1]], banks=["PX%d" % k])
+        y = D if k == 0 else st["t", d]
+        F = slot()
+        op("ve", lambda: V.tensor_tensor(F[0], X(d, k), y[0], sub), reads=[y[1]], writes=[F[1]], banks=["PX%d" % k])
+        if k == 0:
+            t = slot()
+            op("ve", lambda: V.tensor_scalar(t[0], F[0], -1.0, 2 * P + 0.5, mul, add), reads=[F[1]], writes=[t[1]])
+            st["t", d] = t
+            return
+        m = tt(F, D, AluOpType.is_equal)
+        md = tt(m, D, mul)
+        if k < 3:
+            st["t", d] = tt(st["t", d], m, add)
+        st["acc", d] = md if k == 1 else tt(st["acc", d], md, add)
+        if k == 3:
+            acc = st["acc", d]
+            op("ve", lambda: V.tensor_scalar(T["NF%d" % d][:, 64:128], acc[0], float(P), None, add),
+               reads=[acc[1]], writes=[("NF%d" % d, 64, 128)])
+
+    def lists(d):
+        before("po", [("NF%d" % d, 64, 128)], (), ())
+        rid, pid, _se = topo.addr(partner[core])
+        g.remote_dma(T["PF%d" % d][:, 64:128], T["NF%d" % d][:, 64:128], T.sem["l%d" % d], T.sem["sent"], pid, rid,
+                     topo.mask(core, partner[core]))
+        cnt["sent"] += len(topo.engines(core, partner[core]))
+
+    def lst(d, x):
+        return ("NF%d" % d, x // 16) if x < M else ("PF%d" % d, (x - M) // 16)
+
+    def near(d, x, w):
+        b, a = lst(d, x)
+        o = 2 * M * d + x
+        op("ac", lambda: S_.activation(T.A[:, o:o + w], T["W%d" % d][:, 0:WW].indirect(T[b][:, a:a + w // 16]), ident),
+           reads=[("W%d" % d, 0, WW), (b, a, a + w // 16)], writes=[("A", o, o + w)])
+
+    def far(d, x, w):
+        b, a = lst(d, x)
+        a += 64
+        o = 2 * M * d + x
+        op("ve", lambda: V.tensor_tensor(T.S[:, o:o + w], T["W%d" % d][:, 0:WW].indirect(T[b][:, a:a + w // 16]),
+                                         T.A[:, o:o + w], add),
+           reads=[("W%d" % d, 0, WW), (b, a, a + w // 16), ("A", o, o + w)], writes=[("S", o, o + w)])
+
+    def take(d, x, w):
+        o = 2 * M * d + x
+        buf, c = ("W%d" % (d + 1), col(x)) if d < 2 else ("Y", x)
+        op("ve", lambda: V.tensor_tensor(T[buf][:, c:c + w], T["PS%d" % (x // 512)][:, x % 512:x % 512 + w],
+                                         T.S[:, o:o + w], sub),
+           reads=[("S", o, o + w)], writes=[(buf, c, c + w)], banks=["PS%d" % (x // 512)])
+
+    def level(d, k, part):
+        chase("ac", d, k, 0, part)
+        chase("ve", d, k, part, M)
+        flags(d, k - 1)
+        wrap(d, k)
+        if k < 3:
+            parents(d, k)
+
+    send(("ag", 0))
+    digits(0, SEG)
+    rows([0])
+    before("po", [("LO", 0, SEG)], (), ())
+    for k in range(1, len(OPT["ag"])):
+        send(("ag", k))
+    for d in range(ND):
+        op("ve", lambda: V.memset(T["W%d" % d][:, P:WW], 0.0), writes=[("W%d" % d, P, WW)])
+    digits(SEG, ND * SEG)
+    twice(0, 0)
+    twice(0, 1)
+    wrap(0, 0)
+    parents(0, 0)
+    wrap(0, 4)
+    level(0, 1, OPT["p0"])
+    parents(0, 4)
+    level(0, 2, OPT["p0"])
+    level(0, 3, OPT["p0"])
+    rows([1, 2])
+    flags(0, 3)
+    lists(0)
+
+    c = _starts(OPT["ch"])
+    e = OPT["early"]
+    wrap(1, 0)
+    if e:
+        parents(1, 0)
+        flags(1, 0)
+        chase("ac", 1, 1, 0, e)
+    near(0, *c[0])
+    near(0, *c[1])
+    twice(0, 2)
+    far(0, *c[0])
+    far(0, *c[1])
+    near(0, *c[2])
+    take(0, *c[0])
+    take(0, *c[1])
+    send((1, 0))
+    if not e:
+        parents(1, 0)
+    far(0, *c[2])
+    twice(0, 3)
+    chase("ac", 1, 1, e, max(e, OPT["pa"]))
+    near(0, *c[3])
+    take(0, *c[2])
+    send((1, 1))
+    if not e:
+        flags(1, 0)
+    chase("ac", 1, 1, max(e, OPT["pa"]), M)
+    wrap(1, 1)
+    near(0, *c[4])
+    near(0, *c[5])
+    far(0, *c[3])
+    take(0, *c[3])
+    send((1, 2))
+    parents(1, 1)
+    chase("ac", 1, 2, 0, M)
+    wrap(2, 0)
+    wrap(1, 4)
+    twice(1, 0)
+    far(0, *c[4])
+    far(0, *c[5])
+    take(0, *c[4])
+    send((1, 3))
+    take(0, *c[5])
+    send((1, 4))
+    flags(1, 1)
+    wrap(1, 2)
+    parents(1, 2)
+    chase("ac", 1, 3, 0, OPT["p3"])
+    twice(1, 1)
+    parents(2, 0)
+    chase("ve", 1, 3, OPT["p3"], M)
+    wrap(1, 3)
+    chase("ac", 2, 1, 0, M)
+    flags(1, 2)
+    parents(1, 4)
+    flags(1, 3)
+    lists(1)
+    wrap(2, 1)
+    twice(1, 2)
+    twice(1, 3)
+
+    near(1, *c[0])
+    near(1, *c[1])
+    parents(2, 1)
+    far(1, *c[0])
+    far(1, *c[1])
+    near(1, *c[2])
+    take(1, *c[0])
+    take(1, *c[1])
+    send((2, 0))
+    far(1, *c[2])
+    near(1, *c[3])
+    chase("ac", 2, 2, 0, OPT["pb"])
+    take(1, *c[2])
+    send((2, 1))
+    near(1, *c[4])
+    near(1, *c[5])
+    chase("ac", 2, 2, OPT["pb"], M)
+    wrap(2, 2)
+    far(1, *c[3])
+    take(1, *c[3])
+    send((2, 2))
+    far(1, *c[4])
+    far(1, *c[5])
+    take(1, *c[4])
+    send((2, 3))
+    take(1, *c[5])
+    send((2, 4))
+    parents(2, 2)
+    chase("ac", 2, 3, 0, M)
+    twice(2, 0)
+    twice(2, 1)
+    wrap(2, 3)
+    for k in range(4):
+        flags(2, k)
+
+    c = _starts(OPT["last"])
+
+    def store(x, w):
+        take(2, x, w)
+        op("ac", lambda: S_.activation(T.Y2[:, x:x + w], T.Y[:, x:x + w], ident, scale=0.125),
+           reads=[("Y", x, x + w)], writes=[("Y2", x, x + w)])
+        dmas("sy", [(T.y[:, x:x + w], T.Y2[:, x:x + w])], reads=[("Y2", x, x + w)])
+
+    for x, w in c:
+        near(2, x, w)
+    far(2, *c[0])
+    for i in range(1, len(c)):
+        far(2, *c[i])
+        store(*c[i - 1])
+    store(*c[-1])
+
+    for s in cnt:
+        if max(seen[q].get(s, 0) for q in seen) < cnt[s]:
+            wait("po", (s, cnt[s]))

@@ -6,14 +6,13 @@ WW, IWW = P + 8, P + 16
 SEG = P // 16
 FILL = 516
 OPT = {
-    "ag": [128, 384, 384, 128],
+    "ag": [128, 256, 256, 256, 128],
+    "odd": [0, 1, 2],
     "ch": [256, 256, 512, 512, 256, 256],
     "last": [256, 256, 256, 256],
-    "relay": 1,
+    "relay": 2,
     "pen": 128,
-    "p0": 608, "p3": 608, "pa": 512, "pb": 512,
-    "early": 0,
-    "vq": "ac",
+    "p0": 608, "p3": 608, "pc": 640, "pb": 768,
 }
 
 SCRATCH = {
@@ -36,7 +35,7 @@ SCRATCH = {
 for _k in range(4):
     SCRATCH["PS%d" % _k] = ("psum", [128, 512], "float32")
     SCRATCH["PX%d" % _k] = ("psum", [128, 512], "float32")
-SEMAPHORES = (["ve", "ac", "pe", "po", "sent", "a0", "a1", "a2", "l0", "l1"] + ["h%d" % _k for _k in range(24)]
+SEMAPHORES = (["ve", "ac", "pe", "po", "sent", "go", "a0", "a1", "a2", "l0", "l1"] + ["h%d" % _k for _k in range(24)]
               + ["d%d" % _k for _k in range(24)])
 
 
@@ -76,6 +75,11 @@ def _layout(T, topo):
             h = min([x for x in topo.cores_of(partner[c]) if x not in cores and topo.may_write(c, x)],
                     key=lambda x: load.get(x, 0) + (0 if x == inbound[c] else 1 if topo.die(x) == topo.die(c)
                                                     else OPT["pen"]))
+            if k in OPT["odd"] and any(topo.die(x) == topo.die(c) for x in peers[c]):
+                alt = [x for x in range(128) if topo.mates(topo.chip(x), topo.chip(partner[c])) and topo.may_write(c, x)
+                       and topo.may_write(x, partner[c])]
+                if alt:
+                    h = min(alt, key=lambda x: load.get(x, 0))
             load[h] = load.get(h, 0) + w
             off = topo.engines(c, h)
             rest = [e for e in topo.engines(c, peers[c][0]) if e not in off]
@@ -185,8 +189,8 @@ def rank_program(g, core, T, topo):
 
     dmas("sy", [(T.CT[:, 0:SEG], T.tree[:, 0:P])], writes=[("CT", 0, SEG)])
     for a, w in _starts(OPT["ag"]):
-        dmas(OPT["vq"], [(T.W0[:, own + a:own + a + w], T.v[:, a:a + w])], writes=[("W0", own + a, own + a + w)])
-    dmas(OPT["vq"], [(T.CT[:, d * SEG:(d + 1) * SEG], T.tree[:, d * P:(d + 1) * P]) for d in (1, 2)],
+        dmas("ac", [(T.W0[:, own + a:own + a + w], T.v[:, a:a + w])], writes=[("W0", own + a, own + a + w)])
+    dmas("ac", [(T.CT[:, d * SEG:(d + 1) * SEG], T.tree[:, d * P:(d + 1) * P]) for d in (1, 2)],
          writes=[("CT", SEG, ND * SEG)])
     cut = IWW - 5 * FILL
     op("ve", lambda: V.memset(T.IW[:, 0:FILL], float(P)), writes=[("IW", 0, FILL)])
@@ -247,8 +251,6 @@ def rank_program(g, core, T, topo):
            writes=[(b, a, a + 64)], banks=["PX%d" % min(k, 3)])
 
     def chase(q, d, k, lo, hi):
-        if lo == hi:
-            return
         b, a = offs(d, k - 1)
         r = (3 * d + k - 1) * M
         src = T.IW[:, 0:IWW].indirect(T[b][:, a + lo // 16:a + hi // 16])
@@ -332,18 +334,19 @@ def rank_program(g, core, T, topo):
     send(("ag", 0))
     digits(0, SEG)
     rows([0])
-    before("po", [("LO", 0, SEG)], (), ())
+    g.sync.sem_inc(T.sem["go"], 1)
+    g.wait_ge(T.sem["go"], 1)
     for k in range(1, len(OPT["ag"])):
         send(("ag", k))
     for d in range(ND):
         op("ve", lambda: V.memset(T["W%d" % d][:, P:WW], 0.0), writes=[("W%d" % d, P, WW)])
     digits(SEG, ND * SEG)
     twice(0, 0)
-    twice(0, 1)
     wrap(0, 0)
     parents(0, 0)
     wrap(0, 4)
     level(0, 1, OPT["p0"])
+    twice(0, 1)
     parents(0, 4)
     level(0, 2, OPT["p0"])
     level(0, 3, OPT["p0"])
@@ -352,39 +355,31 @@ def rank_program(g, core, T, topo):
     lists(0)
 
     c = _starts(OPT["ch"])
-    e = OPT["early"]
+    twice(0, 2)
     wrap(1, 0)
-    if e:
-        parents(1, 0)
-        flags(1, 0)
-        chase("ac", 1, 1, 0, e)
     near(0, *c[0])
     near(0, *c[1])
-    twice(0, 2)
     far(0, *c[0])
     far(0, *c[1])
     near(0, *c[2])
     take(0, *c[0])
     take(0, *c[1])
     send((1, 0))
-    if not e:
-        parents(1, 0)
+    parents(1, 0)
     far(0, *c[2])
     twice(0, 3)
-    chase("ac", 1, 1, e, max(e, OPT["pa"]))
     near(0, *c[3])
+    chase("ac", 1, 1, 0, M)
     take(0, *c[2])
     send((1, 1))
-    if not e:
-        flags(1, 0)
-    chase("ac", 1, 1, max(e, OPT["pa"]), M)
+    flags(1, 0)
     wrap(1, 1)
     near(0, *c[4])
     near(0, *c[5])
     far(0, *c[3])
+    parents(1, 1)
     take(0, *c[3])
     send((1, 2))
-    parents(1, 1)
     chase("ac", 1, 2, 0, M)
     wrap(2, 0)
     wrap(1, 4)
@@ -403,29 +398,32 @@ def rank_program(g, core, T, topo):
     parents(2, 0)
     chase("ve", 1, 3, OPT["p3"], M)
     wrap(1, 3)
-    chase("ac", 2, 1, 0, M)
+    chase("ac", 2, 1, 0, OPT["pc"])
     flags(1, 2)
     parents(1, 4)
     flags(1, 3)
     lists(1)
-    wrap(2, 1)
     twice(1, 2)
     twice(1, 3)
 
     near(1, *c[0])
     near(1, *c[1])
-    parents(2, 1)
     far(1, *c[0])
     far(1, *c[1])
     near(1, *c[2])
+    chase("ac", 2, 1, OPT["pc"], M)
+    wrap(2, 1)
     take(1, *c[0])
     take(1, *c[1])
     send((2, 0))
     far(1, *c[2])
     near(1, *c[3])
-    chase("ac", 2, 2, 0, OPT["pb"])
+    parents(2, 1)
     take(1, *c[2])
     send((2, 1))
+    chase("ac", 2, 2, 0, OPT["pb"])
+    twice(2, 0)
+    twice(2, 1)
     near(1, *c[4])
     near(1, *c[5])
     chase("ac", 2, 2, OPT["pb"], M)
@@ -441,11 +439,11 @@ def rank_program(g, core, T, topo):
     send((2, 4))
     parents(2, 2)
     chase("ac", 2, 3, 0, M)
-    twice(2, 0)
-    twice(2, 1)
+    flags(2, 0)
+    flags(2, 1)
+    flags(2, 2)
     wrap(2, 3)
-    for k in range(4):
-        flags(2, k)
+    flags(2, 3)
 
     c = _starts(OPT["last"])
 

from concourse.bass import DstId, RemoteDMATransfer
from concourse.mybir import AluOpType, ActivationFunctionType

M, P, ND = 1024, 6144, 3
WW, IWW = P + 8, P + 16
SEG = P // 16
FILL = 516
OPT = {
    "ag": [128, 256, 256, 256, 128],
    "odd": [0, 1, 2],
    "ch": [256, 256, 512, 512, 256, 256],
    "last": [256, 256, 256, 256],
    "relay": 2,
    "pen": 128,
    "p0": 608, "p3": 608, "pc": 640, "pb": 768,
}

SCRATCH = {
    "W0": ("sbuf", [128, WW], "float32"), "W1": ("sbuf", [128, WW], "float32"), "W2": ("sbuf", [128, WW], "float32"),
    "IW": ("sbuf", [128, IWW], "bfloat16"),
    "CT": ("sbuf", [128, ND * SEG], "int32"),
    "HI": ("sbuf", [128, ND * SEG], "bfloat16"), "LO": ("sbuf", [128, ND * SEG], "bfloat16"),
    "R": ("sbuf", [128, 9 * M], "bfloat16"),
    "A": ("sbuf", [128, 5 * M], "float32"), "S": ("sbuf", [128, 5 * M], "float32"),
    "Y": ("sbuf", [128, M], "float32"), "Y2": ("sbuf", [128, M], "float32"),
    "Z": ("sbuf", [128, ND * 144], "bfloat16"),
    "HF": ("sbuf", [128, 32], "bfloat16"), "HG": ("sbuf", [128, 32], "bfloat16"),
    "I2": ("sbuf", [128, 128], "float32"),
    "NF0": ("sbuf", [128, 128], "uint16"), "NF1": ("sbuf", [128, 128], "uint16"), "NF2": ("sbuf", [128, 128], "uint16"),
    "PF0": ("sbuf", [128, 128], "uint16"), "PF1": ("sbuf", [128, 128], "uint16"),
    "Q": ("sbuf", [128, 6 * 64], "uint16"),
    "DI": ("sbuf", [128, 12 * 64], "int32"),
    "SM": ("sbuf", [128, 60 * 64], "float32"),
}
for _k in range(4):
    SCRATCH["PS%d" % _k] = ("psum", [128, 512], "float32")
    SCRATCH["PX%d" % _k] = ("psum", [128, 512], "float32")
SEMAPHORES = (["ve", "ac", "pe", "po", "sent", "go", "a0", "a1", "a2", "l0", "l1"] + ["h%d" % _k for _k in range(24)]
              + ["d%d" % _k for _k in range(24)])


def _starts(widths):
    out, a = [], 0
    for w in widths:
        out.append((a, w))
        a += w
    return out


def _layout(T, topo):
    cores = list(T.cores)
    chips = {}
    for c in cores:
        chips.setdefault(topo.chip(c), []).append(c)
    one, two = list(chips.values())
    partner, peers, inbound = {}, {}, {}
    for mine, other in ((one, two), (two, one)):
        free = [c for c in topo.cores_of(other[0]) if c not in cores]
        for a, b in zip(mine, other):
            partner[a] = b
            peers[a] = [c for c in mine if c != a]
            h = [c for c in free if topo.die(c) == topo.die(a) and topo.may_write(a, c)][0]
            free.remove(h)
            inbound[a] = h
    calls, jobs, load = {c: {} for c in cores}, {}, {}

    def through(h, eng, buf, lo, hi, dsts, sem):
        j = jobs.setdefault(h, [])
        j.append(("h%d" % len(j), len(eng), (buf, lo, hi, [(dsts, topo.engines(h, dsts[0]), sem)])))
        return ([h], eng, j[-1][0])

    for k, (a, w) in enumerate(_starts(OPT["ag"])):
        for c in cores:
            lo = T.rank_of(c) * M + a
            h = min([x for x in topo.cores_of(partner[c]) if x not in cores and topo.may_write(c, x)],
                    key=lambda x: load.get(x, 0) + (0 if x == inbound[c] else 1 if topo.die(x) == topo.die(c)
                                                    else OPT["pen"]))
            if k in OPT["odd"] and any(topo.die(x) == topo.die(c) for x in peers[c]):
                alt = [x for x in range(128) if topo.mates(topo.chip(x), topo.chip(partner[c])) and topo.may_write(c, x)
                       and topo.may_write(x, partner[c])]
                if alt:
                    h = min(alt, key=lambda x: load.get(x, 0))
            load[h] = load.get(h, 0) + w
            off = topo.engines(c, h)
            rest = [e for e in topo.engines(c, peers[c][0]) if e not in off]
            far = through(h, off, "W0", lo, lo + w, [partner[c]] + peers[partner[c]], "a0")
            calls[c]["ag", k] = ("W0", lo, lo + w, [far, (peers[c], rest, "a0")])
    for d in (1, 2):
        for k, (a, w) in enumerate([(0, 512)] + _starts(OPT["ch"])[2:]):
            for c in cores:
                lo = T.rank_of(c) * M + a if a < M else T.rank_of(partner[c]) * M + a - M
                eng, buf, s = topo.engines(c, peers[c][0]), "W%d" % d, "a%d" % d
                way = (through(inbound[partner[c]], eng, buf, lo, lo + w, peers[c], s) if k < OPT["relay"]
                       else (peers[c], eng, s))
                calls[c][d, k] = (buf, lo, lo + w, [way])
    return partner, calls, jobs


def _issue(g, T, topo, call):
    buf, lo, hi, ways = call
    ap, tr = T[buf][:, lo:hi], []
    for dsts, eng, s in ways:
        ids = [DstId(rid=topo.addr(x)[0], pnc=topo.addr(x)[1]) for x in dsts]
        tr.append(RemoteDMATransfer(dst_ids=ids, dma_engine_mask=sum(1 << e for e in eng), remote_sem=T.sem[s],
                                    srcs=[ap], dsts=[ap] * len(dsts)))
    g.remote_dma_fused(tr, local_sem=T.sem["sent"])
    return sum(len(w[1]) for w in ways)


def rank_program(g, core, T, topo):
    partner, calls, jobs = _layout(T, topo)
    rank = T.rank_of(core)
    if rank is None:
        n = 0
        for s, k, call in jobs.get(core, []):
            g.wait_ge(T.sem[s], k)
            n += _issue(g, T, topo, call)
        if n:
            g.wait_ge(T.sem["sent"], n)
        return

    own, par = rank * M, T.rank_of(partner[core]) * M
    Q = {"ve": g.vector, "ac": g.scalar, "pe": g.tensor, "po": g, "sy": g.sync}
    cnt = {"sent": 0}
    seen = {q: {} for q in Q}
    log = {}
    bank = {}
    ndma, nsm = [0], [0]
    add, sub, mul = AluOpType.add, AluOpType.subtract, AluOpType.mult
    ident = ActivationFunctionType.Identity

    def wait(q, tok):
        if seen[q].get(tok[0], 0) < tok[1]:
            Q[q].wait_ge(T.sem[tok[0]], tok[1])
            seen[q][tok[0]] = tok[1]

    def before(q, reads, writes, banks):
        need = {}
        for rs, w in ((reads, False), (writes, True)):
            for (b, lo, hi) in rs:
                for (l2, h2, w2, tok) in log.get(b, []):
                    if l2 < hi and lo < h2 and (w or w2):
                        need[tok[0]] = max(need.get(tok[0], 0), tok[1])
        for b in banks:
            for q2, tok in bank.get(b, {}).items():
                if q2 != q:
                    need[tok[0]] = max(need.get(tok[0], 0), tok[1])
        for s in need:
            wait(q, (s, need[s]))

    def after(q, reads, writes, banks, tok):
        for rs, w in ((reads, False), (writes, True)):
            for (b, lo, hi) in rs:
                log.setdefault(b, []).append((lo, hi, w, tok))
        for b in banks:
            bank.setdefault(b, {})[q] = tok

    def op(q, fn, reads=(), writes=(), banks=()):
        before(q, reads, writes, banks)
        cnt[q] = cnt.get(q, 0) + 1
        fn().then_inc(T.sem[q], 1)
        after(q, reads, writes, banks, (q, cnt[q]))

    def dmas(q, pairs, reads=(), writes=()):
        before(q, reads, writes, ())
        s = "d%d" % ndma[0]
        ndma[0] += 1
        for out, in_ in pairs:
            Q[q].dma_start(out, in_).then_inc(T.sem[s], 16)
        cnt[s] = 16 * len(pairs)
        after(q, reads, writes, (), (s, cnt[s]))

    def send(tag):
        call = calls[core][tag]
        before("po", [call[0:3]], (), ())
        cnt["sent"] += _issue(g, T, topo, call)

    every = [x for c in calls for x in calls[c].values()] + [j[2] for h in jobs for j in jobs[h]]
    here = [(buf, lo, hi, len(eng), s) for (buf, lo, hi, ways) in every for (dsts, eng, s) in ways if core in dsts]
    for buf, lo, hi, n, s in here:
        cnt[s] = cnt.get(s, 0) + n
    for buf, lo, hi, n, s in here:
        after("po", (), [(buf, lo, hi)], (), (s, cnt[s]))
    for d in (0, 1):
        cnt["l%d" % d] = len(topo.engines(partner[core], core))
        after("po", (), [("PF%d" % d, 64, 128)], (), ("l%d" % d, cnt["l%d" % d]))

    V, S_, PE = g.vector, g.scalar, g.tensor

    dmas("sy", [(T.CT[:, 0:SEG], T.tree[:, 0:P])], writes=[("CT", 0, SEG)])
    for a, w in _starts(OPT["ag"]):
        dmas("ac", [(T.W0[:, own + a:own + a + w], T.v[:, a:a + w])], writes=[("W0", own + a, own + a + w)])
    dmas("ac", [(T.CT[:, d * SEG:(d + 1) * SEG], T.tree[:, d * P:(d + 1) * P]) for d in (1, 2)],
         writes=[("CT", SEG, ND * SEG)])
    cut = IWW - 5 * FILL
    op("ve", lambda: V.memset(T.IW[:, 0:FILL], float(P)), writes=[("IW", 0, FILL)])
    op("ve", lambda: V.memset(T.HF[:, :], 0.5), writes=[("HF", 0, 32)])
    op("ve", lambda: V.memset(T.Z[:, :], 0.0), writes=[("Z", 0, 432)])
    op("ve", lambda: V.memset(T.I2[:, :], 2.0), writes=[("I2", 0, 128)])
    op("ve", lambda: V.memset(T.IW[:, FILL:cut], float(P)), writes=[("IW", FILL, cut)])
    for i in range(5):
        a = cut + i * FILL
        op("ac", lambda: S_.activation(T.IW[:, a:a + FILL], T.IW[:, 0:FILL], ident),
           reads=[("IW", 0, FILL)], writes=[("IW", a, a + FILL)])
    op("po", lambda: g.affine_select(T.HG[:, 0:27], T.HF[:, 0:27], [[-2, 3], [-16, 9]], AluOpType.is_ge, 0.0, 0, 1),
       reads=[("HF", 0, 32)], writes=[("HG", 0, 32)])
    op("po", lambda: g.affine_select(T.Z[:, 15::16], T.HG[:, 0:27], [[2, 3], [16, 9]], AluOpType.is_ge, 0.0, 1, -1),
       reads=[("HG", 0, 32)], writes=[("Z", 0, 432)])
    op("po", lambda: g.affine_select(T.I2[:, :], T.I2[:, :], [[-1, 128]], AluOpType.is_equal, 0.0, 0, 1),
       reads=[("I2", 0, 128)], writes=[("I2", 0, 128)])

    def digits(lo, hi):
        op("ve", lambda: V.tensor_copy(T.HI[:, lo:hi], T.CT[:, lo:hi]), reads=[("CT", lo, hi)], writes=[("HI", lo, hi)])
        op("ve", lambda: V.tensor_tensor(T.LO[:, lo:hi], T.CT[:, lo:hi], T.HI[:, lo:hi], sub),
           reads=[("CT", lo, hi), ("HI", lo, hi)], writes=[("LO", lo, hi)])

    def rows(ds):
        pairs = []
        for d in ds:
            pairs.append((T.IW[2 * d::16, 0:P], T.HI[:, d * SEG:(d + 1) * SEG]))
            pairs.append((T.IW[2 * d + 1::16, 0:P], T.LO[:, d * SEG:(d + 1) * SEG]))
        lo, hi = ds[0] * SEG, (ds[-1] + 1) * SEG
        dmas("sy", pairs, reads=[("HI", lo, hi), ("LO", lo, hi)], writes=[("IW", 0, P)])

    def col(x):
        return own + x if x < M else par + x - M

    def twice(d, b):
        c = col(512 * b)
        op("pe", lambda: PE.matmul(T["PS%d" % b][:, 0:512], T.I2[:, :], T["W%d" % d][:, c:c + 512], True, True),
           reads=[("I2", 0, 128), ("W%d" % d, c, c + 512)], banks=["PS%d" % b])

    def X(d, k):
        return T["PX%d" % k][:, 64 * d:64 * d + 64] if k < 4 else T.PX3[:, 192 + 64 * d:256 + 64 * d]

    def wrap(d, k):
        buf, a = ("IW", own) if k == 0 else ("IW", par) if k == 4 else ("R", (3 * d + k - 1) * M)
        reads, banks = [(buf, a, a + M), ("Z", 0, 432)], ["PX%d" % min(k, 3)]
        before("pe", reads, (), banks)
        for o in range(15):
            PE.matmul(X(d, k), T.Z[:, 144 * d + 15 - o:144 * d + 143 - o], T[buf][:, a + o:a + M:16], o == 0, False)
        op("pe", lambda: PE.matmul(X(d, k), T.Z[:, 144 * d:144 * d + 128], T[buf][:, a + 15:a + M:16], False, True),
           reads=reads, banks=banks)

    def offs(d, k):
        return ("NF%d" % d, 0) if k == 0 else ("PF%d" % d, 0) if k == 4 else ("Q", (2 * d + k - 1) * 64)

    def parents(d, k):
        b, a = offs(d, k)
        op("ve", lambda: V.tensor_scalar(T[b][:, a:a + 64], X(d, k), -0.25, None, add),
           writes=[(b, a, a + 64)], banks=["PX%d" % min(k, 3)])

    def chase(q, d, k, lo, hi):
        b, a = offs(d, k - 1)
        r = (3 * d + k - 1) * M
        src = T.IW[:, 0:IWW].indirect(T[b][:, a + lo // 16:a + hi // 16])
        out = T.R[:, r + lo:r + hi]
        fn = (lambda: S_.activation(out, src, ident)) if q == "ac" else (lambda: V.tensor_copy(out, src))
        op(q, fn, reads=[("IW", 0, IWW), (b, a + lo // 16, a + hi // 16)], writes=[("R", r + lo, r + hi)])

    def slot():
        nsm[0] += 1
        a = (nsm[0] - 1) * 64
        return T.SM[:, a:a + 64], ("SM", a, a + 64)

    st = {}

    def tt(x, y, alu):
        o = slot()
        op("ve", lambda: V.tensor_tensor(o[0], x[0], y[0], alu), reads=[x[1], y[1]], writes=[o[1]])
        return o

    def flags(d, k):
        a = (4 * d + k) * 64
        D = (T.DI[:, a:a + 64], ("DI", a, a + 64))
        op("ve", lambda: V.tensor_scalar(D[0], X(d, k), -(P + 0.25), None, add), writes=[D[1]], banks=["PX%d" % k])
        y = D if k == 0 else st["t", d]
        F = slot()
        op("ve", lambda: V.tensor_tensor(F[0], X(d, k), y[0], sub), reads=[y[1]], writes=[F[1]], banks=["PX%d" % k])
        if k == 0:
            t = slot()
            op("ve", lambda: V.tensor_scalar(t[0], F[0], -1.0, 2 * P + 0.5, mul, add), reads=[F[1]], writes=[t[1]])
            st["t", d] = t
            return
        m = tt(F, D, AluOpType.is_equal)
        md = tt(m, D, mul)
        if k < 3:
            st["t", d] = tt(st["t", d], m, add)
        st["acc", d] = md if k == 1 else tt(st["acc", d], md, add)
        if k == 3:
            acc = st["acc", d]
            op("ve", lambda: V.tensor_scalar(T["NF%d" % d][:, 64:128], acc[0], float(P), None, add),
               reads=[acc[1]], writes=[("NF%d" % d, 64, 128)])

    def lists(d):
        before("po", [("NF%d" % d, 64, 128)], (), ())
        rid, pid, _se = topo.addr(partner[core])
        g.remote_dma(T["PF%d" % d][:, 64:128], T["NF%d" % d][:, 64:128], T.sem["l%d" % d], T.sem["sent"], pid, rid,
                     topo.mask(core, partner[core]))
        cnt["sent"] += len(topo.engines(core, partner[core]))

    def lst(d, x):
        return ("NF%d" % d, x // 16) if x < M else ("PF%d" % d, (x - M) // 16)

    def near(d, x, w):
        b, a = lst(d, x)
        o = 2 * M * d + x
        op("ac", lambda: S_.activation(T.A[:, o:o + w], T["W%d" % d][:, 0:WW].indirect(T[b][:, a:a + w // 16]), ident),
           reads=[("W%d" % d, 0, WW), (b, a, a + w // 16)], writes=[("A", o, o + w)])

    def far(d, x, w):
        b, a = lst(d, x)
        a += 64
        o = 2 * M * d + x
        op("ve", lambda: V.tensor_tensor(T.S[:, o:o + w], T["W%d" % d][:, 0:WW].indirect(T[b][:, a:a + w // 16]),
                                         T.A[:, o:o + w], add),
           reads=[("W%d" % d, 0, WW), (b, a, a + w // 16), ("A", o, o + w)], writes=[("S", o, o + w)])

    def take(d, x, w):
        o = 2 * M * d + x
        buf, c = ("W%d" % (d + 1), col(x)) if d < 2 else ("Y", x)
        op("ve", lambda: V.tensor_tensor(T[buf][:, c:c + w], T["PS%d" % (x // 512)][:, x % 512:x % 512 + w],
                                         T.S[:, o:o + w], sub),
           reads=[("S", o, o + w)], writes=[(buf, c, c + w)], banks=["PS%d" % (x // 512)])

    def level(d, k, part):
        chase("ac", d, k, 0, part)
        chase("ve", d, k, part, M)
        flags(d, k - 1)
        wrap(d, k)
        if k < 3:
            parents(d, k)

    send(("ag", 0))
    digits(0, SEG)
    rows([0])
    g.sync.sem_inc(T.sem["go"], 1)
    g.wait_ge(T.sem["go"], 1)
    for k in range(1, len(OPT["ag"])):
        send(("ag", k))
    for d in range(ND):
        op("ve", lambda: V.memset(T["W%d" % d][:, P:WW], 0.0), writes=[("W%d" % d, P, WW)])
    digits(SEG, ND * SEG)
    twice(0, 0)
    wrap(0, 0)
    parents(0, 0)
    wrap(0, 4)
    level(0, 1, OPT["p0"])
    twice(0, 1)
    parents(0, 4)
    level(0, 2, OPT["p0"])
    level(0, 3, OPT["p0"])
    rows([1, 2])
    flags(0, 3)
    lists(0)

    c = _starts(OPT["ch"])
    twice(0, 2)
    wrap(1, 0)
    near(0, *c[0])
    near(0, *c[1])
    far(0, *c[0])
    far(0, *c[1])
    near(0, *c[2])
    take(0, *c[0])
    take(0, *c[1])
    send((1, 0))
    parents(1, 0)
    far(0, *c[2])
    twice(0, 3)
    near(0, *c[3])
    chase("ac", 1, 1, 0, M)
    take(0, *c[2])
    send((1, 1))
    flags(1, 0)
    wrap(1, 1)
    near(0, *c[4])
    near(0, *c[5])
    far(0, *c[3])
    parents(1, 1)
    take(0, *c[3])
    send((1, 2))
    chase("ac", 1, 2, 0, M)
    wrap(2, 0)
    wrap(1, 4)
    twice(1, 0)
    far(0, *c[4])
    far(0, *c[5])
    take(0, *c[4])
    send((1, 3))
    take(0, *c[5])
    send((1, 4))
    flags(1, 1)
    wrap(1, 2)
    parents(1, 2)
    chase("ac", 1, 3, 0, OPT["p3"])
    twice(1, 1)
    parents(2, 0)
    chase("ve", 1, 3, OPT["p3"], M)
    wrap(1, 3)
    chase("ac", 2, 1, 0, OPT["pc"])
    flags(1, 2)
    parents(1, 4)
    flags(1, 3)
    lists(1)
    twice(1, 2)
    twice(1, 3)

    near(1, *c[0])
    near(1, *c[1])
    far(1, *c[0])
    far(1, *c[1])
    near(1, *c[2])
    chase("ac", 2, 1, OPT["pc"], M)
    wrap(2, 1)
    take(1, *c[0])
    take(1, *c[1])
    send((2, 0))
    far(1, *c[2])
    near(1, *c[3])
    parents(2, 1)
    take(1, *c[2])
    send((2, 1))
    chase("ac", 2, 2, 0, OPT["pb"])
    twice(2, 0)
    twice(2, 1)
    near(1, *c[4])
    near(1, *c[5])
    chase("ac", 2, 2, OPT["pb"], M)
    wrap(2, 2)
    far(1, *c[3])
    take(1, *c[3])
    send((2, 2))
    far(1, *c[4])
    far(1, *c[5])
    take(1, *c[4])
    send((2, 3))
    take(1, *c[5])
    send((2, 4))
    parents(2, 2)
    chase("ac", 2, 3, 0, M)
    flags(2, 0)
    flags(2, 1)
    flags(2, 2)
    wrap(2, 3)
    flags(2, 3)

    c = _starts(OPT["last"])

    def store(x, w):
        take(2, x, w)
        op("ac", lambda: S_.activation(T.Y2[:, x:x + w], T.Y[:, x:x + w], ident, scale=0.125),
           reads=[("Y", x, x + w)], writes=[("Y2", x, x + w)])
        dmas("sy", [(T.y[:, x:x + w], T.Y2[:, x:x + w])], reads=[("Y2", x, x + w)])

    for x, w in c:
        near(2, x, w)
    far(2, *c[0])
    for i in range(1, len(c)):
        far(2, *c[i])
        store(*c[i - 1])
    store(*c[-1])

    for s in cnt:
        if max(seen[q].get(s, 0) for q in seen) < cnt[s]:
            wait("po", (s, cnt[s]))
